import numpy as np, ml_dtypes
CORES = [6,14,22,30,38,46,54,62,70,142,150,158]
N = 12
import mx_ref
NC, KB = 128, 1
BF = ml_dtypes.bfloat16
def cut(t, i, w=512):
    return t[:, w * i:w * i + w]
def term(a, B):
    return np.stack([mx_ref.matmul(mx_ref.quantize(cut(a, i)), B) for i in range(4)], axis=2).reshape(128, -1)
def setup_inputs(rng):
    def f(*shape):
        return mx_ref.flush((rng.standard_normal(shape, dtype=np.float32) * np.exp2(rng.integers(-2, 3, shape[:-1] + (1,)))).astype(BF))
    return {"a": f(N, 128, 4 * 512), "b": f(N, 128, KB * 4 * NC)}
def setup_inputs_blocks(rng):
    d = setup_inputs(rng)
    for k in ("a", "b"): d[k] = mx_ref.spread(d[k], rng, 2)
    return d
def setup_inputs_wide(rng):
    d = setup_inputs(rng)
    for k in ("a", "b"): d[k] = mx_ref.flush((d[k].astype(np.float32) * np.exp2(rng.integers(-4, 5, (N, 1, 1))).astype(np.float32)).astype(BF))
    return d
def setup_inputs_lossless(rng):
    a = np.zeros((N, 128, 4 * 128, 4), np.float32)
    for r in range(N):
        k = rng.integers(0, 512, size=4 * 128)
        a[r, k // 4, np.arange(4 * 128), k % 4] = 1.0
    size = np.repeat(2.0 ** rng.integers(-4, 5, size=(1, 1, (KB * 4 * NC) // 4)), 4, axis=2)
    b = rng.integers(-1, 2, size=(N, 128, KB * 4 * NC)) * size
    return {"a": a.reshape(N, 128, 4 * 512).astype(BF), "b": b.astype(np.float32).astype(BF)}
def reference(a, b):
    y = np.zeros((N, 128, KB * 4 * NC), np.float32)
    for k in range(KB):
        y[:, :, 4 * NC * k:4 * NC * k + 4 * NC] = mx_ref.total([term(a[r], mx_ref.quantize(cut(b[r], k, 4 * NC))) for r in range(N)])
    return {"y": y}

@@ -1,0 +1,216 @@
+from concourse.bass import DstId, RemoteDMATransfer
+from concourse.mybir import dt, AluOpType, ActivationFunctionType
+
+W = 128
+E = 4 * W
+BANK = 512
+SLOTS = 8
+HA, HB, SA = 5, 6, 7
+ORDER = (2, 0, 3, 1)
+ON_VECTOR = (2, 3)
+
+SCRATCH = {
+    "ta": ("sbuf", [128, 4 * E], "bfloat16"),
+    "tb": ("sbuf", [128, E], "bfloat16"),
+    "eye": ("sbuf", [128, E + 8], "bfloat16"),
+    "qa": ("sbuf", [128, 4 * W], "float8_e4m3fn_x4"),
+    "qas": ("sbuf", [128, 4 * W], "uint8"),
+    "qb": ("sbuf", [128, W], "float8_e4m3fn_x4"),
+    "qbs": ("sbuf", [128, W], "uint8"),
+    "sel": ("sbuf", [128, 4 * W], "float8_e4m3fn_x4"),
+    "sels": ("sbuf", [128, 4 * W], "uint8"),
+    "h1": ("sbuf", [128, E], "bfloat16"),
+    "h2": ("sbuf", [128, E], "bfloat16"),
+    "q1": ("sbuf", [128, W], "float8_e4m3fn_x4"),
+    "q1s": ("sbuf", [128, W], "uint8"),
+    "q2": ("sbuf", [128, W], "float8_e4m3fn_x4"),
+    "q2s": ("sbuf", [128, W], "uint8"),
+    "lc": ("sbuf", [128, SLOTS * W], "float8_e4m3fn_x4"),
+    "ls": ("sbuf", [128, SLOTS * W], "uint8"),
+    "out": ("sbuf", [128, E], "float32"),
+    "acc": ("psum", [128, 4 * BANK], "float32"),
+    "fin": ("psum", [128, 4 * BANK], "float32"),
+}
+SEMAPHORES = (["lb", "la0", "la1", "fill", "eyed", "selq", "qbd", "qad0", "qad1", "sent", "stored"]
+              + ["land_c%d" % k for k in range(SLOTS)] + ["land_s%d" % k for k in range(SLOTS)]
+              + ["m%d_%d" % (ph, b) for ph in range(3) for b in range(4)]
+              + ["v%d_%d" % (ph, b) for ph in range(3) for b in range(4)]
+              + ["q%dd" % ph for ph in (1, 2)])
+
+
+def make_plan(T, topo):
+    cores = list(T.cores)
+    hosts = sorted({topo.host(c) for c in cores}, key=lambda h: -sum(topo.host(c) == h for c in cores))
+    home = [c for c in cores if topo.host(c) == hosts[0]]
+    away = [c for c in cores if topo.host(c) != hosts[0]]
+    first = [c for c in home if c == home[0] or topo.same_plane(c, home[0])]
+    other = [c for c in home if c not in first]
+    A, B = (first, other) if len(first) >= len(other) else (other, first)
+    pairs = [(a, b) for a in A for b in B if topo.mates(a, b)][:3]
+    rootA, rootB = [p[0] for p in pairs], [p[1] for p in pairs]
+    leafA, leafB = [c for c in A if c not in rootA], [c for c in B if c not in rootB]
+    gates = [(a, b) for a in away for b in away if topo.mates(a, b) and topo.same_plane(a, A[0])][0]
+    rest = [c for c in away if c not in gates]
+
+    serves = [[], list(leafA), list(leafB)]
+    enterA, enterB = leafA[-1], leafB[-1]
+
+    plan = {}
+    for plane, roots, leaves, half, mine in ((A, rootA, leafA, HA, 0), (B, rootB, leafB, HB, 1)):
+        gate, enter = gates[mine], (enterA, enterB)[mine]
+        for c in plane:
+            p = {"slot1": plane.index(c), "hop1": [[d for d in roots if d != c]], "hop2": [], "fwd": [], "slot2": half}
+            if c in roots:
+                k = roots.index(c)
+                p["sum"] = [plane.index(d) for d in roots + leaves if d != c]
+                p["final"] = [HB if half == HA else HA, SA]
+                if k == 0:
+                    p["hop2"].append([gate])
+                p["hop2"].append([pairs[k][1 - mine]] + serves[k])
+            else:
+                p["sum"] = None
+                p["final"] = [HA, HB, SA]
+                if c == enter:
+                    p["fwd"].append((SA, [d for d in plane if d != c]))
+            plan[c] = p
+    for mine, gate in enumerate(gates):
+        half = (HA, HB)[mine]
+        plan[gate] = {"slot1": away.index(gate), "hop1": [[gates[1 - mine]]], "slot2": SA,
+                      "sum": [away.index(d) for d in away if d != gate],
+                      "hop2": [[(enterA, enterB)[mine]]] + ([rest] if mine == 1 else []),
+                      "fwd": [(half, [gates[1 - mine]] + rest)],
+                      "final": [half, HB if half == HA else HA]}
+    for c in rest:
+        plan[c] = {"slot1": away.index(c), "hop1": [[gates[0]], [gates[1]]], "slot2": None, "sum": None, "hop2": [],
+                   "fwd": [], "final": [SA, HA, HB]}
+    return plan
+
+
+def rank_program(g, core, T, topo):
+    if T.rank_of(core) is None:
+        return
+    me = make_plan(T, topo)[core]
+    s = T.sem
+    calls = [0]
+
+    def tile(t, k):
+        return t[:, k * W:(k + 1) * W]
+
+    def bank(t, b):
+        return t[:, b * BANK:b * BANK + W]
+
+    def send(src, land, sem, dsts):
+        mask = 0xFFFF
+        for d in dsts:
+            mask &= topo.mask(core, d)
+        ids = []
+        for d in dsts:
+            rid, pid = topo.addr(d, core)
+            ids.append(DstId(rid=rid, pnc=pid))
+        if len(dsts) == 1:
+            g.remote_dma(land, src, sem, s.sent, ids[0].pnc, ids[0].rid, mask)
+        else:
+            g.remote_dma_fused([RemoteDMATransfer(dst_ids=ids, dma_engine_mask=mask, remote_sem=sem, srcs=[src],
+                                                  dsts=[land for d in dsts])], local_sem=s.sent)
+        calls[0] += bin(mask).count("1")
+
+    def send_codes(q, slot, dsts):
+        send(q.bitcast(dt.uint8), tile(T.lc, slot).bitcast(dt.uint8), s["land_c%d" % slot], dsts)
+
+    def send_scales(q, slot, dsts):
+        send(q, tile(T.ls, slot), s["land_s%d" % slot], dsts)
+
+    g.sync.dma_start(T.tb[:], T.b[:]).then_inc(s.lb, 16)
+    g.scalar.dma_start(T.ta[:, 0:2 * E], T.a[:, 0:2 * E]).then_inc(s.la0, 16)
+    g.sync.dma_start(T.ta[:, 2 * E:4 * E], T.a[:, 2 * E:4 * E]).then_inc(s.la1, 16)
+
+    g.vector.memset(T.eye[:], 0.0).then_inc(s.fill, 1)
+    g.wait_ge(s.fill, 1)
+    g.affine_select(T.eye[:], T.eye[:], [[-1, E + 8]], AluOpType.not_equal, 1.0, 3, 4).then_inc(s.eyed, 1)
+    g.vector.wait_ge(s.eyed, 1)
+    for b in range(4):
+        g.vector.quantize_mx(tile(T.sel, b), tile(T.sels, b), T.eye[:, 3 - b:3 - b + E]).then_inc(s.selq, 1)
+
+    g.vector.wait_ge(s.lb, 16)
+    g.vector.quantize_mx(T.qb[:], T.qbs[:], T.tb[:]).then_inc(s.qbd, 1)
+    for h in range(2):
+        g.vector.wait_ge(s["la%d" % h], 16)
+        g.vector.quantize_mx(T.qa[:, 2 * h * W:2 * (h + 1) * W], T.qas[:, 2 * h * W:2 * (h + 1) * W],
+                             T.ta[:, 2 * h * E:2 * (h + 1) * E]).then_inc(s["qad%d" % h], 1)
+
+    g.tensor.wait_ge(s.qbd, 1)
+    for h in range(2):
+        g.tensor.wait_ge(s["qad%d" % h], 1)
+        for i in (2 * h, 2 * h + 1):
+            g.tensor.matmul_mx(bank(T.acc, i), tile(T.qa, i), tile(T.qas, i), T.qb[:], T.qbs[:], True,
+                               True).then_inc(s["m0_%d" % i], 1)
+
+    def copy_out(ph, src, dst, on_vector):
+        for b in range(4):
+            b = ORDER[b] if ph else b
+            out = dst[:, b:E:4]
+            if b in on_vector:
+                g.vector.wait_ge(s["m%d_%d" % (ph, b)], 1)
+                g.vector.tensor_copy(out, bank(src, b)).then_inc(s["v%d_%d" % (ph, b)], 1)
+            else:
+                g.scalar.wait_ge(s["m%d_%d" % (ph, b)], 1)
+                g.scalar.activation(out, bank(src, b), ActivationFunctionType.Copy).then_inc(s["v%d_%d" % (ph, b)], 1)
+
+    def pack(ph, h, q, qs):
+        for b in range(4):
+            g.vector.wait_ge(s["v%d_%d" % (ph - 1, b)], 1)
+        g.vector.quantize_mx(q[:], qs[:], h[:]).then_inc(s["q%dd" % ph], 1)
+
+    def add_tiles(ph, out, own, slots):
+        first = True
+        if own is not None:
+            for b in ORDER:
+                g.tensor.matmul_mx(bank(out, b), tile(T.sel, b), tile(T.sels, b), own[0][:], own[1][:], True, False)
+            first = False
+        for n, k in enumerate(slots):
+            g.tensor.wait_ge(s["land_c%d" % k], 8)
+            g.tensor.wait_ge(s["land_s%d" % k], 8)
+            last = n == len(slots) - 1
+            for b in ORDER:
+                mm = g.tensor.matmul_mx(bank(out, b), tile(T.sel, b), tile(T.sels, b), tile(T.lc, k), tile(T.ls, k),
+                                        first, last)
+                if last:
+                    mm.then_inc(s["m%d_%d" % (ph, b)], 1)
+            first = False
+
+    copy_out(0, T.acc, T.h1, (2,))
+    pack(1, T.h1, T.q1, T.q1s)
+    g.wait_ge(s.q1d, 1)
+    for dsts in me["hop1"]:
+        send_codes(T.q1[:], me["slot1"], dsts)
+        send_scales(T.q1s[:], me["slot1"], dsts)
+
+    g.tensor.wait_ge(s.selq, 4)
+    own = None
+    if me["sum"] is not None:
+        g.tensor.wait_ge(s.q1d, 1)
+        for b in range(4):
+            g.tensor.wait_ge(s["v0_%d" % b], 1)
+        add_tiles(1, T.acc, (T.q1, T.q1s), me["sum"])
+        copy_out(1, T.acc, T.h2, ON_VECTOR)
+        pack(2, T.h2, T.q2, T.q2s)
+        g.wait_ge(s.q2d, 1)
+        for dsts in me["hop2"]:
+            send_codes(T.q2[:], me["slot2"], dsts)
+            send_scales(T.q2s[:], me["slot2"], dsts)
+        g.tensor.wait_ge(s.q2d, 1)
+        own = (T.q2, T.q2s)
+
+    for slot, dsts in me["fwd"]:
+        g.wait_ge(s["land_c%d" % slot], 8)
+        send_codes(tile(T.lc, slot), slot, dsts)
+        g.wait_ge(s["land_s%d" % slot], 8)
+        send_scales(tile(T.ls, slot), slot, dsts)
+
+    add_tiles(2, T.fin, own, me["final"])
+    copy_out(2, T.fin, T.out, ON_VECTOR)
+    for b in range(4):
+        g.sync.wait_ge(s["v2_%d" % b], 1)
+    g.sync.dma_start(T.y[:], T.out[:]).then_inc(s.stored, 16)
+    g.sync.wait_ge(s.stored, 16)
+    g.wait_ge(s.sent, calls[0])

@@ -6,7 +6,7 @@ E = 4 * W
 BANK = 512
 SLOTS = 8
 HA, HB, SA = 5, 6, 7
-ORDER = (2, 0, 3, 1)
+ORDER = (0, 2, 1, 3)
 ON_VECTOR = (2, 3)
 
 SCRATCH = {
@@ -31,11 +31,11 @@ SCRATCH = {
     "acc": ("psum", [128, 4 * BANK], "float32"),
     "fin": ("psum", [128, 4 * BANK], "float32"),
 }
-SEMAPHORES = (["lb", "la0", "la1", "fill", "eyed", "selq", "qbd", "qad0", "qad1", "sent", "stored"]
+SEMAPHORES = (["lb", "la0", "la1", "fill", "eyed", "selq", "qbd", "sent", "stored", "q1d", "q2d"]
               + ["land_c%d" % k for k in range(SLOTS)] + ["land_s%d" % k for k in range(SLOTS)]
+              + ["qad%d" % i for i in range(4)]
               + ["m%d_%d" % (ph, b) for ph in range(3) for b in range(4)]
-              + ["v%d_%d" % (ph, b) for ph in range(3) for b in range(4)]
-              + ["q%dd" % ph for ph in (1, 2)])
+              + ["v%d_%d" % (ph, b) for ph in range(3) for b in range(4)])
 
 
 def make_plan(T, topo):
@@ -52,37 +52,37 @@ def make_plan(T, topo):
     gates = [(a, b) for a in away for b in away if topo.mates(a, b) and topo.same_plane(a, A[0])][0]
     rest = [c for c in away if c not in gates]
 
-    serves = [[], list(leafA), list(leafB)]
-    enterA, enterB = leafA[-1], leafB[-1]
+    serves = [leafB, leafA[:1], leafA[1:]]
+    enter = (leafA[-1], leafB[-1])
 
     plan = {}
-    for plane, roots, leaves, half, mine in ((A, rootA, leafA, HA, 0), (B, rootB, leafB, HB, 1)):
-        gate, enter = gates[mine], (enterA, enterB)[mine]
+    for mine, (plane, roots, leaves) in enumerate(((A, rootA, leafA), (B, rootB, leafB))):
+        half, otherhalf = (HA, HB) if mine == 0 else (HB, HA)
         for c in plane:
-            p = {"slot1": plane.index(c), "hop1": [[d for d in roots if d != c]], "hop2": [], "fwd": [], "slot2": half}
+            p = {"slot1": plane.index(c), "slot2": half, "hop1": [[d for d in roots if d != c]], "hop2": [], "fwd": []}
             if c in roots:
                 k = roots.index(c)
                 p["sum"] = [plane.index(d) for d in roots + leaves if d != c]
-                p["final"] = [HB if half == HA else HA, SA]
                 if k == 0:
-                    p["hop2"].append([gate])
+                    p["hop2"].append([gates[mine]])
                 p["hop2"].append([pairs[k][1 - mine]] + serves[k])
+                p["final"] = [otherhalf, SA]
             else:
                 p["sum"] = None
-                p["final"] = [HA, HB, SA]
-                if c == enter:
+                p["final"] = [SA, HB, HA] if c in enter else [HB, HA, SA]
+                if c == enter[mine]:
                     p["fwd"].append((SA, [d for d in plane if d != c]))
             plan[c] = p
     for mine, gate in enumerate(gates):
-        half = (HA, HB)[mine]
-        plan[gate] = {"slot1": away.index(gate), "hop1": [[gates[1 - mine]]], "slot2": SA,
-                      "sum": [away.index(d) for d in away if d != gate],
-                      "hop2": [[(enterA, enterB)[mine]]] + ([rest] if mine == 1 else []),
-                      "fwd": [(half, [gates[1 - mine]] + rest)],
-                      "final": [half, HB if half == HA else HA]}
+        half, otherhalf = (HA, HB) if mine == 0 else (HB, HA)
+        mate = gates[1 - mine]
+        plan[gate] = {"slot1": away.index(gate), "hop1": [[mate]], "slot2": SA,
+                      "sum": [away.index(d) for d in [mate] + rest],
+                      "hop2": [[enter[mine]]] + ([rest] if mine == 1 else []), "fwd": [(half, rest + [mate])],
+                      "final": [half, otherhalf]}
     for c in rest:
         plan[c] = {"slot1": away.index(c), "hop1": [[gates[0]], [gates[1]]], "slot2": None, "sum": None, "hop2": [],
-                   "fwd": [], "final": [SA, HA, HB]}
+                   "fwd": [], "final": [SA, HB, HA]}
     return plan
 
 
@@ -133,17 +133,16 @@ def rank_program(g, core, T, topo):
 
     g.vector.wait_ge(s.lb, 16)
     g.vector.quantize_mx(T.qb[:], T.qbs[:], T.tb[:]).then_inc(s.qbd, 1)
-    for h in range(2):
-        g.vector.wait_ge(s["la%d" % h], 16)
-        g.vector.quantize_mx(T.qa[:, 2 * h * W:2 * (h + 1) * W], T.qas[:, 2 * h * W:2 * (h + 1) * W],
-                             T.ta[:, 2 * h * E:2 * (h + 1) * E]).then_inc(s["qad%d" % h], 1)
+    for i in range(4):
+        if i % 2 == 0:
+            g.vector.wait_ge(s["la%d" % (i // 2)], 16)
+        g.vector.quantize_mx(tile(T.qa, i), tile(T.qas, i), T.ta[:, i * E:(i + 1) * E]).then_inc(s["qad%d" % i], 1)
 
     g.tensor.wait_ge(s.qbd, 1)
-    for h in range(2):
-        g.tensor.wait_ge(s["qad%d" % h], 1)
-        for i in (2 * h, 2 * h + 1):
-            g.tensor.matmul_mx(bank(T.acc, i), tile(T.qa, i), tile(T.qas, i), T.qb[:], T.qbs[:], True,
-                               True).then_inc(s["m0_%d" % i], 1)
+    for i in range(4):
+        g.tensor.wait_ge(s["qad%d" % i], 1)
+        g.tensor.matmul_mx(bank(T.acc, i), tile(T.qa, i), tile(T.qas, i), T.qb[:], T.qbs[:], True,
+                           True).then_inc(s["m0_%d" % i], 1)
 
     def copy_out(ph, src, dst, on_vector):
         for b in range(4):
@@ -168,8 +167,8 @@ def rank_program(g, core, T, topo):
                 g.tensor.matmul_mx(bank(out, b), tile(T.sel, b), tile(T.sels, b), own[0][:], own[1][:], True, False)
             first = False
         for n, k in enumerate(slots):
-            g.tensor.wait_ge(s["land_c%d" % k], 8)
             g.tensor.wait_ge(s["land_s%d" % k], 8)
+            g.tensor.wait_ge(s["land_c%d" % k], 8)
             last = n == len(slots) - 1
             for b in ORDER:
                 mm = g.tensor.matmul_mx(bank(out, b), tile(T.sel, b), tile(T.sels, b), tile(T.lc, k), tile(T.ls, k),
@@ -178,12 +177,12 @@ def rank_program(g, core, T, topo):
                     mm.then_inc(s["m%d_%d" % (ph, b)], 1)
             first = False
 
-    copy_out(0, T.acc, T.h1, (2,))
+    copy_out(0, T.acc, T.h1, (3,))
     pack(1, T.h1, T.q1, T.q1s)
     g.wait_ge(s.q1d, 1)
     for dsts in me["hop1"]:
-        send_codes(T.q1[:], me["slot1"], dsts)
         send_scales(T.q1s[:], me["slot1"], dsts)
+        send_codes(T.q1[:], me["slot1"], dsts)
 
     g.tensor.wait_ge(s.selq, 4)
     own = None
@@ -196,16 +195,16 @@ def rank_program(g, core, T, topo):
         pack(2, T.h2, T.q2, T.q2s)
         g.wait_ge(s.q2d, 1)
         for dsts in me["hop2"]:
-            send_codes(T.q2[:], me["slot2"], dsts)
             send_scales(T.q2s[:], me["slot2"], dsts)
+            send_codes(T.q2[:], me["slot2"], dsts)
         g.tensor.wait_ge(s.q2d, 1)
         own = (T.q2, T.q2s)
 
     for slot, dsts in me["fwd"]:
-        g.wait_ge(s["land_c%d" % slot], 8)
-        send_codes(tile(T.lc, slot), slot, dsts)
         g.wait_ge(s["land_s%d" % slot], 8)
         send_scales(tile(T.ls, slot), slot, dsts)
+        g.wait_ge(s["land_c%d" % slot], 8)
+        send_codes(tile(T.lc, slot), slot, dsts)
 
     add_tiles(2, T.fin, own, me["final"])
     copy_out(2, T.fin, T.out, ON_VECTOR)

from concourse.bass import DstId, RemoteDMATransfer
from concourse.mybir import dt, AluOpType, ActivationFunctionType

W = 128
E = 4 * W
BANK = 512
SLOTS = 8
HA, HB, SA = 5, 6, 7
ORDER = (0, 2, 1, 3)
ON_VECTOR = (2, 3)

SCRATCH = {
    "ta": ("sbuf", [128, 4 * E], "bfloat16"),
    "tb": ("sbuf", [128, E], "bfloat16"),
    "eye": ("sbuf", [128, E + 8], "bfloat16"),
    "qa": ("sbuf", [128, 4 * W], "float8_e4m3fn_x4"),
    "qas": ("sbuf", [128, 4 * W], "uint8"),
    "qb": ("sbuf", [128, W], "float8_e4m3fn_x4"),
    "qbs": ("sbuf", [128, W], "uint8"),
    "sel": ("sbuf", [128, 4 * W], "float8_e4m3fn_x4"),
    "sels": ("sbuf", [128, 4 * W], "uint8"),
    "h1": ("sbuf", [128, E], "bfloat16"),
    "h2": ("sbuf", [128, E], "bfloat16"),
    "q1": ("sbuf", [128, W], "float8_e4m3fn_x4"),
    "q1s": ("sbuf", [128, W], "uint8"),
    "q2": ("sbuf", [128, W], "float8_e4m3fn_x4"),
    "q2s": ("sbuf", [128, W], "uint8"),
    "lc": ("sbuf", [128, SLOTS * W], "float8_e4m3fn_x4"),
    "ls": ("sbuf", [128, SLOTS * W], "uint8"),
    "out": ("sbuf", [128, E], "float32"),
    "acc": ("psum", [128, 4 * BANK], "float32"),
    "fin": ("psum", [128, 4 * BANK], "float32"),
}
SEMAPHORES = (["lb", "la0", "la1", "fill", "eyed", "selq", "qbd", "sent", "stored", "q1d", "q2d"]
              + ["land_c%d" % k for k in range(SLOTS)] + ["land_s%d" % k for k in range(SLOTS)]
              + ["qad%d" % i for i in range(4)]
              + ["m%d_%d" % (ph, b) for ph in range(3) for b in range(4)]
              + ["v%d_%d" % (ph, b) for ph in range(3) for b in range(4)])


def make_plan(T, topo):
    cores = list(T.cores)
    hosts = sorted({topo.host(c) for c in cores}, key=lambda h: -sum(topo.host(c) == h for c in cores))
    home = [c for c in cores if topo.host(c) == hosts[0]]
    away = [c for c in cores if topo.host(c) != hosts[0]]
    first = [c for c in home if c == home[0] or topo.same_plane(c, home[0])]
    other = [c for c in home if c not in first]
    A, B = (first, other) if len(first) >= len(other) else (other, first)
    pairs = [(a, b) for a in A for b in B if topo.mates(a, b)][:3]
    rootA, rootB = [p[0] for p in pairs], [p[1] for p in pairs]
    leafA, leafB = [c for c in A if c not in rootA], [c for c in B if c not in rootB]
    gates = [(a, b) for a in away for b in away if topo.mates(a, b) and topo.same_plane(a, A[0])][0]
    rest = [c for c in away if c not in gates]

    serves = [leafB, leafA[:1], leafA[1:]]
    enter = (leafA[-1], leafB[-1])

    plan = {}
    for mine, (plane, roots, leaves) in enumerate(((A, rootA, leafA), (B, rootB, leafB))):
        half, otherhalf = (HA, HB) if mine == 0 else (HB, HA)
        for c in plane:
            p = {"slot1": plane.index(c), "slot2": half, "hop1": [[d for d in roots if d != c]], "hop2": [], "fwd": []}
            if c in roots:
                k = roots.index(c)
                p["sum"] = [plane.index(d) for d in roots + leaves if d != c]
                if k == 0:
                    p["hop2"].append([gates[mine]])
                p["hop2"].append([pairs[k][1 - mine]] + serves[k])
                p["final"] = [otherhalf, SA]
            else:
                p["sum"] = None
                p["final"] = [SA, HB, HA] if c in enter else [HB, HA, SA]
                if c == enter[mine]:
                    p["fwd"].append((SA, [d for d in plane if d != c]))
            plan[c] = p
    for mine, gate in enumerate(gates):
        half, otherhalf = (HA, HB) if mine == 0 else (HB, HA)
        mate = gates[1 - mine]
        plan[gate] = {"slot1": away.index(gate), "hop1": [[mate]], "slot2": SA,
                      "sum": [away.index(d) for d in [mate] + rest],
                      "hop2": [[enter[mine]]] + ([rest] if mine == 1 else []), "fwd": [(half, rest + [mate])],
                      "final": [half, otherhalf]}
    for c in rest:
        plan[c] = {"slot1": away.index(c), "hop1": [[gates[0]], [gates[1]]], "slot2": None, "sum": None, "hop2": [],
                   "fwd": [], "final": [SA, HB, HA]}
    return plan


def rank_program(g, core, T, topo):
    if T.rank_of(core) is None:
        return
    me = make_plan(T, topo)[core]
    s = T.sem
    calls = [0]

    def tile(t, k):
        return t[:, k * W:(k + 1) * W]

    def bank(t, b):
        return t[:, b * BANK:b * BANK + W]

    def send(src, land, sem, dsts):
        mask = 0xFFFF
        for d in dsts:
            mask &= topo.mask(core, d)
        ids = []
        for d in dsts:
            rid, pid = topo.addr(d, core)
            ids.append(DstId(rid=rid, pnc=pid))
        if len(dsts) == 1:
            g.remote_dma(land, src, sem, s.sent, ids[0].pnc, ids[0].rid, mask)
        else:
            g.remote_dma_fused([RemoteDMATransfer(dst_ids=ids, dma_engine_mask=mask, remote_sem=sem, srcs=[src],
                                                  dsts=[land for d in dsts])], local_sem=s.sent)
        calls[0] += bin(mask).count("1")

    def send_codes(q, slot, dsts):
        send(q.bitcast(dt.uint8), tile(T.lc, slot).bitcast(dt.uint8), s["land_c%d" % slot], dsts)

    def send_scales(q, slot, dsts):
        send(q, tile(T.ls, slot), s["land_s%d" % slot], dsts)

    g.sync.dma_start(T.tb[:], T.b[:]).then_inc(s.lb, 16)
    g.scalar.dma_start(T.ta[:, 0:2 * E], T.a[:, 0:2 * E]).then_inc(s.la0, 16)
    g.sync.dma_start(T.ta[:, 2 * E:4 * E], T.a[:, 2 * E:4 * E]).then_inc(s.la1, 16)

    g.vector.memset(T.eye[:], 0.0).then_inc(s.fill, 1)
    g.wait_ge(s.fill, 1)
    g.affine_select(T.eye[:], T.eye[:], [[-1, E + 8]], AluOpType.not_equal, 1.0, 3, 4).then_inc(s.eyed, 1)
    g.vector.wait_ge(s.eyed, 1)
    for b in range(4):
        g.vector.quantize_mx(tile(T.sel, b), tile(T.sels, b), T.eye[:, 3 - b:3 - b + E]).then_inc(s.selq, 1)

    g.vector.wait_ge(s.lb, 16)
    g.vector.quantize_mx(T.qb[:], T.qbs[:], T.tb[:]).then_inc(s.qbd, 1)
    for i in range(4):
        if i % 2 == 0:
            g.vector.wait_ge(s["la%d" % (i // 2)], 16)
        g.vector.quantize_mx(tile(T.qa, i), tile(T.qas, i), T.ta[:, i * E:(i + 1) * E]).then_inc(s["qad%d" % i], 1)

    g.tensor.wait_ge(s.qbd, 1)
    for i in range(4):
        g.tensor.wait_ge(s["qad%d" % i], 1)
        g.tensor.matmul_mx(bank(T.acc, i), tile(T.qa, i), tile(T.qas, i), T.qb[:], T.qbs[:], True,
                           True).then_inc(s["m0_%d" % i], 1)

    def copy_out(ph, src, dst, on_vector):
        for b in range(4):
            b = ORDER[b] if ph else b
            out = dst[:, b:E:4]
            if b in on_vector:
                g.vector.wait_ge(s["m%d_%d" % (ph, b)], 1)
                g.vector.tensor_copy(out, bank(src, b)).then_inc(s["v%d_%d" % (ph, b)], 1)
            else:
                g.scalar.wait_ge(s["m%d_%d" % (ph, b)], 1)
                g.scalar.activation(out, bank(src, b), ActivationFunctionType.Copy).then_inc(s["v%d_%d" % (ph, b)], 1)

    def pack(ph, h, q, qs):
        for b in range(4):
            g.vector.wait_ge(s["v%d_%d" % (ph - 1, b)], 1)
        g.vector.quantize_mx(q[:], qs[:], h[:]).then_inc(s["q%dd" % ph], 1)

    def add_tiles(ph, out, own, slots):
        first = True
        if own is not None:
            for b in ORDER:
                g.tensor.matmul_mx(bank(out, b), tile(T.sel, b), tile(T.sels, b), own[0][:], own[1][:], True, False)
            first = False
        for n, k in enumerate(slots):
            g.tensor.wait_ge(s["land_s%d" % k], 8)
            g.tensor.wait_ge(s["land_c%d" % k], 8)
            last = n == len(slots) - 1
            for b in ORDER:
                mm = g.tensor.matmul_mx(bank(out, b), tile(T.sel, b), tile(T.sels, b), tile(T.lc, k), tile(T.ls, k),
                                        first, last)
                if last:
                    mm.then_inc(s["m%d_%d" % (ph, b)], 1)
            first = False

    copy_out(0, T.acc, T.h1, (3,))
    pack(1, T.h1, T.q1, T.q1s)
    g.wait_ge(s.q1d, 1)
    for dsts in me["hop1"]:
        send_scales(T.q1s[:], me["slot1"], dsts)
        send_codes(T.q1[:], me["slot1"], dsts)

    g.tensor.wait_ge(s.selq, 4)
    own = None
    if me["sum"] is not None:
        g.tensor.wait_ge(s.q1d, 1)
        for b in range(4):
            g.tensor.wait_ge(s["v0_%d" % b], 1)
        add_tiles(1, T.acc, (T.q1, T.q1s), me["sum"])
        copy_out(1, T.acc, T.h2, ON_VECTOR)
        pack(2, T.h2, T.q2, T.q2s)
        g.wait_ge(s.q2d, 1)
        for dsts in me["hop2"]:
            send_scales(T.q2s[:], me["slot2"], dsts)
            send_codes(T.q2[:], me["slot2"], dsts)
        g.tensor.wait_ge(s.q2d, 1)
        own = (T.q2, T.q2s)

    for slot, dsts in me["fwd"]:
        g.wait_ge(s["land_s%d" % slot], 8)
        send_scales(tile(T.ls, slot), slot, dsts)
        g.wait_ge(s["land_c%d" % slot], 8)
        send_codes(tile(T.lc, slot), slot, dsts)

    add_tiles(2, T.fin, own, me["final"])
    copy_out(2, T.fin, T.out, ON_VECTOR)
    for b in range(4):
        g.sync.wait_ge(s["v2_%d" % b], 1)
    g.sync.dma_start(T.y[:], T.out[:]).then_inc(s.stored, 16)
    g.sync.wait_ge(s.stored, 16)
    g.wait_ge(s.sent, calls[0])
